import numpy as np
import ml_dtypes

BF16 = ml_dtypes.bfloat16


def bf(x):
    return np.asarray(x, np.float32).astype(BF16)


def f32(x):
    return np.asarray(x, np.float32)


def f64(x):
    return np.asarray(x).astype(np.float64)


def striped(idx):
    return np.concatenate([l.reshape(-1, 16).T for l in idx])


def rows(idx, k):
    return np.tile(np.repeat(idx, 16, axis=0), (k // (16 * 8), 1))


def look(tab, idx):
    return np.take_along_axis(f64(tab), rows(idx, len(tab)), axis=1)


K, S, V, N = 256, 2048, 1536, 1536


def silu(v):
    return v / (1.0 + np.exp(-v))


def setup_inputs():
    return {"tab": f32(np.random.standard_normal((2, K, S))), "offs": striped(np.stack([np.random.permutation(S)[:N] for _ in range(8)]))}


def reference(tab, offs):
    idx = np.stack([g.T.reshape(-1) for g in np.split(offs, 8)])
    x = ((look(tab[0], idx) - 0.125) * 1.5) * (silu(look(tab[1], idx)))
    return x

@@ -1,0 +1,52 @@
+import concourse.mybir as mybir
+
+F32 = mybir.dt.float32
+U16 = mybir.dt.uint16
+ALU = mybir.AluOpType
+SILU = mybir.ActivationFunctionType.Silu
+
+P = 128
+PIECE = 512
+OFFSETS_PER_COLUMN = 16
+
+
+def tile_lookup_vg_nrmsilu_out_kernel(tc, tab, offs, out):
+    nc = tc.nc
+    _, rows, places = tab.shape
+    n = out.shape[1]
+    blocks = rows // P
+    pieces = n // PIECE
+    piece_columns = PIECE // OFFSETS_PER_COLUMN
+
+    with (
+        tc.tile_pool(name="held", bufs=1) as held,
+        tc.tile_pool(name="work", bufs=blocks * pieces) as work,
+    ):
+        lists = held.tile([P, n // OFFSETS_PER_COLUMN], U16, name="lists")
+        nc.sync.dma_start(lists[:], offs)
+
+        value_tables = []
+        gate_tables = []
+        for b in range(blocks):
+            block_rows = slice(b * P, (b + 1) * P)
+            value_table = held.tile([P, places], F32, name=f"value_table{b}")
+            nc.sync.dma_start(value_table[:], tab[0, block_rows, :])
+            value_tables.append(value_table)
+            gate_table = held.tile([P, places], F32, name=f"gate_table{b}")
+            nc.sync.dma_start(gate_table[:], tab[1, block_rows, :])
+            gate_tables.append(gate_table)
+
+        for b in range(blocks):
+            for k in range(pieces):
+                piece_list = lists[:, k * piece_columns : (k + 1) * piece_columns]
+
+                value = work.tile([P, PIECE], F32, name="value")
+                nc.vector.tensor_scalar(
+                    value[:], value_tables[b][:].indirect(piece_list), 0.125, 1.5, ALU.subtract, ALU.mult
+                )
+                gate = work.tile([P, PIECE], F32, name="gate")
+                nc.scalar.activation(gate[:], gate_tables[b][:].indirect(piece_list), SILU)
+
+                product = work.tile([P, PIECE], F32, name="product")
+                nc.vector.tensor_tensor(product[:], value[:], gate[:], ALU.mult)
+                nc.sync.dma_start(out[b * P : (b + 1) * P, k * PIECE : (k + 1) * PIECE], product[:])

@@ -22,6 +22,11 @@ def tile_lookup_vg_nrmsilu_out_kernel(tc, tab, offs, out):
         tc.tile_pool(name="held", bufs=1) as held,
         tc.tile_pool(name="work", bufs=blocks * pieces) as work,
     ):
+        zeros = held.tile([P, 1], F32, name="zeros")
+        nc.vector.memset(zeros[:], 0.0)
+        warm = held.tile([P, 1], F32, name="warm")
+        nc.scalar.activation(warm[:], zeros[:], SILU)
+
         lists = held.tile([P, n // OFFSETS_PER_COLUMN], U16, name="lists")
         nc.sync.dma_start(lists[:], offs)
 
@@ -48,5 +53,6 @@ def tile_lookup_vg_nrmsilu_out_kernel(tc, tab, offs, out):
                 nc.scalar.activation(gate[:], gate_tables[b][:].indirect(piece_list), SILU)
 
                 product = work.tile([P, PIECE], F32, name="product")
-                nc.vector.tensor_tensor(product[:], value[:], gate[:], ALU.mult)
+                product_engine = nc.vector if b == blocks - 1 else nc.gpsimd
+                product_engine.tensor_tensor(product[:], value[:], gate[:], ALU.mult)
                 nc.sync.dma_start(out[b * P : (b + 1) * P, k * PIECE : (k + 1) * PIECE], product[:])

import concourse.mybir as mybir

F32 = mybir.dt.float32
U16 = mybir.dt.uint16
ALU = mybir.AluOpType
SILU = mybir.ActivationFunctionType.Silu

P = 128
PIECE = 512
OFFSETS_PER_COLUMN = 16


def tile_lookup_vg_nrmsilu_out_kernel(tc, tab, offs, out):
    nc = tc.nc
    _, rows, places = tab.shape
    n = out.shape[1]
    blocks = rows // P
    pieces = n // PIECE
    piece_columns = PIECE // OFFSETS_PER_COLUMN

    with (
        tc.tile_pool(name="held", bufs=1) as held,
        tc.tile_pool(name="work", bufs=blocks * pieces) as work,
    ):
        zeros = held.tile([P, 1], F32, name="zeros")
        nc.vector.memset(zeros[:], 0.0)
        warm = held.tile([P, 1], F32, name="warm")
        nc.scalar.activation(warm[:], zeros[:], SILU)

        lists = held.tile([P, n // OFFSETS_PER_COLUMN], U16, name="lists")
        nc.sync.dma_start(lists[:], offs)

        value_tables = []
        gate_tables = []
        for b in range(blocks):
            block_rows = slice(b * P, (b + 1) * P)
            value_table = held.tile([P, places], F32, name=f"value_table{b}")
            nc.sync.dma_start(value_table[:], tab[0, block_rows, :])
            value_tables.append(value_table)
            gate_table = held.tile([P, places], F32, name=f"gate_table{b}")
            nc.sync.dma_start(gate_table[:], tab[1, block_rows, :])
            gate_tables.append(gate_table)

        for b in range(blocks):
            for k in range(pieces):
                piece_list = lists[:, k * piece_columns : (k + 1) * piece_columns]

                value = work.tile([P, PIECE], F32, name="value")
                nc.vector.tensor_scalar(
                    value[:], value_tables[b][:].indirect(piece_list), 0.125, 1.5, ALU.subtract, ALU.mult
                )
                gate = work.tile([P, PIECE], F32, name="gate")
                nc.scalar.activation(gate[:], gate_tables[b][:].indirect(piece_list), SILU)

                product = work.tile([P, PIECE], F32, name="product")
                product_engine = nc.vector if b == blocks - 1 else nc.gpsimd
                product_engine.tensor_tensor(product[:], value[:], gate[:], ALU.mult)
                nc.sync.dma_start(out[b * P : (b + 1) * P, k * PIECE : (k + 1) * PIECE], product[:])
